import numpy as np
import ml_dtypes


def mxq(x, axis, fmt="e4m3"):
    dtype, down = {"e4m3": (ml_dtypes.float8_e4m3fn, 7), "e5m2": (ml_dtypes.float8_e5m2, 14)}[fmt]
    v = np.moveaxis(np.asarray(x, np.float32).astype(ml_dtypes.bfloat16).astype(np.float64), axis, -1)
    blocks = v.reshape(v.shape[:-1] + (-1, 32))
    amax = np.abs(blocks).max(-1, keepdims=True)
    byte = np.maximum(np.where(amax > 0, np.frexp(amax)[1] - 1 + 127, 0) - down, 1)
    scale = np.exp2(byte - 127.0)
    codes = (blocks / scale).astype(np.float32).astype(dtype).astype(np.float64)
    return np.moveaxis((codes * scale).reshape(v.shape), -1, axis)


WIDE = False


def mx_kscale(k):
    if not WIDE:
        return np.ones(k)
    levels = np.array([10, -10, 5, -5, 0])
    if k % 512:
        return np.exp2(np.random.permutation(np.resize(levels, k // 32))).repeat(32)
    a = np.empty((k // 512, 16))
    for p in range(k // 512):
        a[p, :8] = np.random.permutation(np.resize(levels, 8))
        for g in range(8):
            far = levels[np.abs(levels - a[p, g]) >= 10]
            a[p, g + 8] = far[np.random.randint(len(far))]
    return np.exp2(a.ravel()).repeat(32)


def f64(x):
    return np.asarray(x).astype(np.float64)


def striped(idx):
    return np.tile(np.asarray(idx).reshape(-1, 16).T, (8, 1)).astype(np.uint16)


def unstriped(offs):
    return offs[:16].T.reshape(-1).astype(np.int64)


E2M1 = np.array([0.0, 0.5, 1.0, 1.5, 2.0, 3.0, 4.0, 6.0, -0.0, -0.5, -1.0, -1.5, -2.0, -3.0, -4.0, -6.0])


def pack_weight(w, fmt):
    k, n = w.shape
    w = f64(np.asarray(w, np.float32).astype(ml_dtypes.bfloat16)).reshape(k // 32, 32, n)
    amax = np.abs(w).max(1)
    if fmt == "e4m3":
        byte = np.frexp(amax)[1] - 1 + 127 - 7
    else:
        mant, ex = np.frexp(amax / 6.0)
        byte = np.where(mant > 0.5, ex, ex - 1) + 127
    byte = np.clip(np.where(amax > 0, byte, 1), 1, 254)
    scaled = (w * np.exp2(127.0 - byte)[:, None, :]).reshape(k, n).astype(np.float32)
    by_word = np.ascontiguousarray(scaled.reshape(k // 512, 128, 4, n).transpose(0, 1, 3, 2))
    if fmt == "e4m3":
        words = by_word.astype(ml_dtypes.float8_e4m3fn).view(np.uint8)
    else:
        c = by_word.astype(ml_dtypes.float4_e2m1fn).view(np.uint8) & 0xF
        words = (c[..., 0::2] | (c[..., 1::2] << 4)).reshape(k // 512, 128, 2 * n)
    return np.ascontiguousarray(words), np.ascontiguousarray(byte.astype(np.uint8).reshape(k // 512, 16, n))


def unpack_weight(words, scales, fmt):
    g, _, n = scales.shape
    words = np.ascontiguousarray(words).reshape(g, 128, n, -1)
    if fmt == "e4m3":
        vals = words.view(ml_dtypes.float8_e4m3fn).astype(np.float64)
    else:
        nib = np.empty((g, 128, n, 4), np.uint8)
        nib[..., 0::2] = words & 0xF
        nib[..., 1::2] = words >> 4
        vals = E2M1[nib]
    vals = vals * np.repeat(np.exp2(scales.astype(np.float64) - 127.0), 8, axis=1)[..., None]
    return vals.transpose(0, 1, 3, 2).reshape(g * 512, n)


D, E, T, I, U, Q = 512, 512, 1024, 512, 2048, 128


def setup_inputs():
    n = np.random.standard_normal
    idx = np.random.permutation(T)[:I]
    idx2 = np.random.permutation(U)[:I]
    fd = mx_kscale(D)
    fe = mx_kscale(E)
    cvalsp = pack_weight(n((E, T)) / fe[:, None], "e4m3")
    return {
        "query": (n((D, Q)) * 0.6 / np.sqrt(D) * fd[:, None]).astype(np.float32),
        "keys": (n((D, T)) / fd[:, None]).astype(np.float32),
        "gout": (n((E, Q)) * 1 / np.sqrt(E) * fe[:, None]).astype(np.float32),
        "cvals_words": cvalsp[0],
        "cvals_scales": cvalsp[1],
        "corr": (n((E, U)) / fe[:, None]).astype(np.float32),
        "us": (np.random.uniform(0.5, 2.0, (1, I))).astype(np.float32),
        "dquery": (n((D, Q)) * 1.0 / np.sqrt(D) * fd[:, None]).astype(np.float32),
        "base": (0.5 * n((Q, T))).astype(np.float32),
        "offs": striped(idx),
        "offs2": striped(idx2),
    }


def reference(query, keys, gout, cvals_words, cvals_scales, corr, us, dquery, base, offs, offs2):
    idx = unstriped(offs)
    idx2 = unstriped(offs2)
    cvalsu = unpack_weight(cvals_words, cvals_scales, "e4m3")
    queryq = mxq(f64(query), 0, "e4m3")
    keysq = mxq(f64(keys), 0, "e4m3")
    a = queryq.T @ keysq
    dqueryq = mxq(f64(dquery), 0, "e4m3")
    ta = dqueryq.T @ keysq
    m1 = np.max(a, axis=1, keepdims=True)
    p = np.exp(a - m1)
    z = np.sum(p, axis=1, keepdims=True)
    px = np.exp(a[:, idx] - m1)
    goutq = mxq(f64(gout), 0, "e4m3")
    c0 = goutq.T @ cvalsu
    corridx2q = mxq(f64(corr)[:, idx2], 0, "e4m3")
    c1 = goutq.T @ corridx2q
    dpx = 1.0 / z * c1 * f64(us)
    dz = (np.sum(p * c0, axis=1, keepdims=True) + np.sum(px * f64(us) * c1, axis=1, keepdims=True)) / np.square(z) * (-1.0)
    dp = 1.0 / z * c0 + dz
    xp = ta * p
    xz = np.sum(xp, axis=1, keepdims=True)
    xpx = ta[:, idx] * px
    xdpx = xz * 1.0 / np.square(z) * (-1.0) * c1 * f64(us)
    xdz = (np.sum(xp * c0, axis=1, keepdims=True) + np.sum(xpx * f64(us) * c1, axis=1, keepdims=True) - xz * z * 2.0 * (np.sum(p * c0, axis=1, keepdims=True) + np.sum(px * f64(us) * c1, axis=1, keepdims=True)) / np.square(z)) / np.square(z) * (-1.0)
    xdp = xz * 1.0 / np.square(z) * (-1.0) * c0 + xdz
    xe1 = xdpx * px + xpx * dpx
    xs1 = np.zeros((Q, T))
    xs1[:, idx] = xe1
    xda = xdp * p + xp * dp + xs1
    y = xda * 1024.0 + f64(base)
    return y

@@ -1,0 +1,246 @@
+from contextlib import ExitStack
+
+import concourse.mybir as mybir
+from concourse.masks import make_identity
+
+D, E, T, I, U, Q = 512, 512, 1024, 512, 2048, 128
+FLOPS = 2 * Q * (2 * D * T + E * T + E * I)
+
+F32 = mybir.dt.float32
+BF16 = mybir.dt.bfloat16
+I32 = mybir.dt.int32
+U32 = mybir.dt.uint32
+U16 = mybir.dt.uint16
+U8 = mybir.dt.uint8
+FP8X4 = mybir.dt.float8_e4m3fn_x4
+ALU = mybir.AluOpType
+ACT = mybir.ActivationFunctionType
+AXIS = mybir.AxisListType
+
+P = 128
+PACK = 4
+BANK = 512
+OUT_SCALE = 1024.0
+KEY_CHUNK = 256
+KEY_CHUNKS = tuple((c0, KEY_CHUNK) for c0 in range(0, T, KEY_CHUNK))
+HALVES = (slice(0, BANK), slice(BANK, T))
+
+
+def tile_attend_hvvaluepatch_kernel(tc, query, keys, gout, cvals_words, cvals_scales, corr, us, dquery, base, offs, offs2, out):
+    nc = tc.nc
+
+    def weave_views(dst, src):
+        return (dst.rearrange("p (c i) t -> p c t i", i=4), src.rearrange("p t (c i) -> p c t i", i=4))
+
+    def weave_vector(dst, src):
+        d, s = weave_views(dst, src)
+        nc.vector.tensor_copy(out=d, in_=s)
+
+    def weave_scalar(dst, src):
+        d, s = weave_views(dst, src)
+        nc.scalar.activation(out=d, in_=s, func=ACT.Copy)
+
+    def quantize(codes, scales, woven):
+        nc.vector.quantize_mx(out=codes.bitcast(FP8X4), scales=scales, in_=woven.rearrange("p w t -> p (w t)"))
+
+    def product(bank, l_codes, l_scales, r_codes, r_scales):
+        nc.tensor.matmul_mx(out=bank, lhsT=l_codes.bitcast(FP8X4), lhsT_scale=l_scales,
+                            rhs=r_codes.bitcast(FP8X4), rhs_scale=r_scales, start=True, stop=True)
+
+    with ExitStack() as ctx:
+        lists = ctx.enter_context(tc.tile_pool(name="lists", bufs=1))
+        sb = ctx.enter_context(tc.tile_pool(name="sb", bufs=1))
+        ps = ctx.enter_context(tc.psum_pool(name="ps", bufs=1))
+
+        def f32(name, width):
+            return sb.tile([P, width], F32, name=name, align_bytes=64)
+
+        warm = f32("warm", 1)
+        nc.vector.memset(warm[:], 0.0)
+        warm_out = f32("warm_out", 1)
+        nc.scalar.activation(out=warm_out[:], in_=warm[:], func=ACT.Exp)
+        cv_scales = sb.tile([P, T], U8, name="cv_scales", align_bytes=64)
+        ident = sb.tile([P, P], F32, name="ident")
+        make_identity(nc, ident[:])
+        nc.gpsimd.memset(cv_scales[:].bitcast(I32), 0)
+        a_sb = f32("a_sb", T)
+        xs1 = f32("xs1", T)
+        nc.vector.memset(xs1[:], 0.0)
+
+        q_raw = sb.tile([P, PACK, Q], F32, name="q_raw")
+        nc.sync.dma_start(out=q_raw[:], in_=query.rearrange("(p t) q -> p t q", t=PACK))
+        keys_v = keys.rearrange("(p t) n -> p t n", t=PACK)
+        k_raw = []
+        for c, (c0, w) in enumerate(KEY_CHUNKS):
+            kt = sb.tile([P, PACK, w], F32, name="k_raw%d" % c)
+            nc.sync.dma_start(out=kt[:], in_=keys_v[:, :, c0:c0 + w])
+            k_raw.append(kt)
+            if c == 0:
+                us_col = sb.tile([P, PACK], F32, name="us_col")
+                nc.sync.dma_start(out=us_col[:], in_=us.rearrange("o (p t) -> (o p) t", t=PACK))
+                idx = lists.tile([P, I // 16], U16, name="idx")
+                nc.sync.dma_start(idx[:], offs)
+        dq_raw = sb.tile([P, PACK, Q], F32, name="dq_raw")
+        nc.sync.dma_start(out=dq_raw[:], in_=dquery.rearrange("(p t) q -> p t q", t=PACK))
+        go_raw = sb.tile([P, PACK, Q], F32, name="go_raw")
+        nc.sync.dma_start(out=go_raw[:], in_=gout.rearrange("(p t) q -> p t q", t=PACK))
+        for g in range(4):
+            nc.gpsimd.dma_start(out=cv_scales[32 * g:32 * g + 4, :].bitcast(I32),
+                                in_=cvals_scales[0, 4 * g:4 * g + 4, :].bitcast(I32))
+        corr_v = corr.rearrange("(p t) u -> t p u", t=PACK)
+        planes = [sb.tile([P, U], F32, name="corr%d" % t) for t in range(PACK)]
+        nc.sync.dma_start(out=planes[0][:], in_=corr_v[0])
+        idx2 = lists.tile([P, I // 16], U16, name="idx2")
+        nc.sync.dma_start(idx2[:], offs2)
+        nc.sync.dma_start(out=planes[1][:], in_=corr_v[1])
+        cv_words = sb.tile([P, T], U32, name="cv_words", align_bytes=64)
+        nc.sync.dma_start(out=cv_words[:].bitcast(I32),
+                          in_=cvals_words[0].rearrange("p n t -> p (n t)").bitcast(I32))
+        nc.sync.dma_start(out=planes[2][:], in_=corr_v[2])
+        nc.sync.dma_start(out=planes[3][:], in_=corr_v[3])
+        base_sb = f32("base_sb", T)
+        nc.sync.dma_start(out=base_sb[:], in_=base)
+
+        q_bf = sb.tile([P, Q, PACK], BF16, name="q_bf", align_bytes=64)
+        q_codes = sb.tile([P, Q], U32, name="q_codes", align_bytes=64)
+        q_scales = sb.tile([P, Q], U8, name="q_scales", align_bytes=64)
+        weave_vector(q_bf[:], q_raw[:])
+        quantize(q_codes[:], q_scales[:], q_bf[:])
+        k_bf = sb.tile([P, T, PACK], BF16, name="k_bf", align_bytes=64)
+        k_codes = sb.tile([P, T], U32, name="k_codes", align_bytes=64)
+        k_scales = sb.tile([P, T], U8, name="k_scales", align_bytes=64)
+        row_max = None
+        for c, (c0, w) in enumerate(KEY_CHUNKS):
+            wv = w * 5 // 8 if c == len(KEY_CHUNKS) - 1 else w * 3 // 8
+            weave_vector(k_bf[:, c0:c0 + wv, :], k_raw[c][:, :, :wv])
+            weave_scalar(k_bf[:, c0 + wv:c0 + w, :], k_raw[c][:, :, wv:])
+            quantize(k_codes[:, c0:c0 + w], k_scales[:, c0:c0 + w], k_bf[:, c0:c0 + w, :])
+            a_ps = ps.tile([P, w], F32, name="a_ps%d" % c, tag="a_ps%d" % (c % 2))
+            product(a_ps[:], q_codes[:], q_scales[:], k_codes[:, c0:c0 + w], k_scales[:, c0:c0 + w])
+            if c == len(KEY_CHUNKS) - 1:
+                dq_bf = sb.tile([P, Q, PACK], BF16, name="dq_bf", align_bytes=64)
+                dq_codes = sb.tile([P, Q], U32, name="dq_codes", align_bytes=64)
+                dq_scales = sb.tile([P, Q], U8, name="dq_scales", align_bytes=64)
+                weave_scalar(dq_bf[:], dq_raw[:])
+                quantize(dq_codes[:], dq_scales[:], dq_bf[:])
+            new_max = f32("row_max%d" % c, 1)
+            nc.vector.tensor_scalar(out=a_sb[:, c0:c0 + w], in0=a_ps[:], scalar1=0.0,
+                                    scalar2=None if row_max is None else row_max[:],
+                                    op0=ALU.add, op1=ALU.max, accum_out=new_max[:])
+            row_max = new_max
+        neg_max = f32("neg_max", 1)
+        nc.scalar.activation(out=neg_max[:], in_=row_max[:], func=ACT.Copy, scale=-1.0)
+
+        ax = f32("ax", I)
+        nc.vector.tensor_copy(out=ax[:], in_=a_sb[:].indirect(idx[:]))
+        p = f32("p", T)
+        zh = f32("zh", 2)
+        xz = f32("xz", 2)
+        for h, cols in enumerate(HALVES):
+            nc.scalar.activation(out=p[:, cols], in_=a_sb[:, cols], func=ACT.Exp, bias=neg_max[:], accum_out=zh[:, h:h + 1])
+        z = f32("z", 1)
+        nc.gpsimd.tensor_tensor(out=z[:], in0=zh[:, 0:1], in1=zh[:, 1:2], op=ALU.add)
+        r = f32("r", 1)
+        nc.vector.reciprocal(out=r[:], in_=z[:])
+        big_r = f32("big_r", 1)
+        nc.gpsimd.tensor_scalar(out=big_r[:], in0=r[:], scalar1=OUT_SCALE, scalar2=1.0, op0=ALU.mult, op1=ALU.mult)
+        neg_r = f32("neg_r", 1)
+        nc.gpsimd.tensor_scalar(out=neg_r[:], in0=r[:], scalar1=-1.0, scalar2=1.0, op0=ALU.mult, op1=ALU.mult)
+        neg_rr = f32("neg_rr", 1)
+        nc.gpsimd.tensor_scalar(out=neg_rr[:], in0=r[:], scalar1=r[:], scalar2=-OUT_SCALE, op0=ALU.mult, op1=ALU.mult)
+        ta_sb = f32("ta_sb", T)
+        picked_words = f32("picked_words", I)
+        picked = picked_words[:].bitcast(BF16).rearrange("p (t i) -> p t i", t=2)
+        for h, cols in enumerate(HALVES):
+            ta_ps = ps.tile([P, BANK], F32, name="ta_ps%d" % h)
+            product(ta_ps[:], dq_codes[:], dq_scales[:], k_codes[:, cols], k_scales[:, cols])
+            nc.vector.scalar_tensor_tensor(out=picked_words[:], in0=ta_ps[:], scalar=1.0, in1=p[:, cols],
+                                           op0=ALU.mult, op1=ALU.mult, accum_out=xz[:, h:h + 1])
+            nc.scalar.activation(out=ta_sb[:, cols], in_=ta_ps[:], func=ACT.Copy)
+        shift = f32("shift", 1)
+        nc.gpsimd.tensor_scalar(out=shift[:], in0=xz[:, 0:1], scalar1=xz[:, 1:2], scalar2=neg_rr[:], op0=ALU.add, op1=ALU.mult)
+
+        tax = sb.tile([P, T], F32, name="tax", align_bytes=64)[:, :I]
+        nc.vector.tensor_copy(out=tax, in_=ta_sb[:].indirect(idx[:]))
+
+        u = f32("u", T)
+        pu = f32("pu", T)
+        for cols in HALVES:
+            nc.scalar.activation(out=u[:, cols], in_=ta_sb[:, cols], func=ACT.Identity, scale=big_r[:], bias=shift[:])
+            nc.gpsimd.tensor_tensor(out=pu[:, cols], in0=u[:, cols], in1=p[:, cols], op=ALU.mult)
+        us_ps = ps.tile([P, PACK, P], F32, name="us_ps", tag="listed")
+        for t in range(PACK):
+            nc.tensor.transpose(us_ps[:, t, :], us_col[:, t:t + 1].to_broadcast([P, P]), ident[:])
+        us_row = f32("us_row", I)
+        nc.scalar.activation(out=us_row[:].rearrange("q (p t) -> q p t", t=PACK),
+                             in_=us_ps[:].rearrange("q t p -> q p t"), func=ACT.Copy)
+
+        px = f32("px", I)
+        nc.scalar.activation(out=px[:], in_=ax[:], func=ACT.Exp, bias=neg_max[:])
+        ux = f32("ux", I)
+        nc.scalar.activation(out=ux[:], in_=tax, func=ACT.Identity, scale=big_r[:], bias=shift[:])
+        w_val = f32("w_val", I)
+        nc.gpsimd.tensor_tensor(out=w_val[:], in0=px[:], in1=us_row[:], op=ALU.mult)
+        w_dir = f32("w_dir", I)
+        nc.gpsimd.tensor_tensor(out=w_dir[:], in0=w_val[:], in1=ux[:], op=ALU.mult)
+
+        go_bf = sb.tile([P, Q, PACK], BF16, name="go_bf", align_bytes=64)
+        go_codes = sb.tile([P, Q], U32, name="go_codes", align_bytes=64)
+        go_scales = sb.tile([P, Q], U8, name="go_scales", align_bytes=64)
+        weave_scalar(go_bf[:], go_raw[:])
+        quantize(go_codes[:], go_scales[:], go_bf[:])
+
+        for t in range(2):
+            nc.vector.tensor_copy(out=picked[:, t, :], in_=planes[t][:].indirect(idx2[:]))
+        yb = sb.tile([P, T], F32, name="yb", tag="tax", align_bytes=64)
+        c_bf = yb[:].bitcast(BF16).rearrange("p (i t) -> p i t", t=PACK)
+        weave_scalar(c_bf[:, :, :2], picked)
+
+        nc.vector.tensor_copy(out=c_bf[:, :, 2], in_=planes[2][:].indirect(idx2[:]))
+
+        y = f32("y", T)
+        k_sum = f32("k_sum", 3)
+        s_sum = f32("s_sum", 3)
+        c0_ps = [ps.tile([P, BANK], F32, name="c0_ps%d" % h) for h in range(2)]
+        for h, cols in enumerate(HALVES):
+            product(c0_ps[h][:], go_codes[:], go_scales[:], cv_words[:, cols], cv_scales[:, cols])
+            nc.vector.scalar_tensor_tensor(out=y[:, cols], in0=c0_ps[h][:], scalar=1.0, in1=pu[:, cols],
+                                           op0=ALU.mult, op1=ALU.mult, accum_out=k_sum[:, h:h + 1])
+
+        nc.vector.tensor_copy(out=c_bf[:, :, 3], in_=planes[3][:].indirect(idx2[:]))
+        c_codes = sb.tile([P, I], U32, name="c_codes", align_bytes=64)
+        c_scales = sb.tile([P, I], U8, name="c_scales", align_bytes=64)
+        quantize(c_codes[:], c_scales[:], c_bf)
+        c1_ps = ps.tile([P, I], F32, name="c1_ps", tag="listed")
+        product(c1_ps[:], go_codes[:], go_scales[:], c_codes[:], c_scales[:])
+        xe1 = f32("xe1", I)
+        junk2 = f32("junk2", BANK)
+        nc.vector.scalar_tensor_tensor(out=junk2[:], in0=c1_ps[:], scalar=1.0, in1=w_val[:],
+                                       op0=ALU.mult, op1=ALU.mult, accum_out=s_sum[:, 2:3])
+        nc.vector.scalar_tensor_tensor(out=xe1[:], in0=c1_ps[:], scalar=1.0, in1=w_dir[:],
+                                       op0=ALU.mult, op1=ALU.mult, accum_out=k_sum[:, 2:3])
+        for h, cols in enumerate(HALVES):
+            nc.vector.scalar_tensor_tensor(out=yb[:, HALVES[1]], in0=c0_ps[h][:], scalar=1.0, in1=p[:, cols],
+                                           op0=ALU.mult, op1=ALU.mult, accum_out=s_sum[:, h:h + 1])
+        for cols in HALVES:
+            nc.gpsimd.tensor_tensor(out=yb[:, cols], in0=y[:, cols], in1=base_sb[:, cols], op=ALU.add)
+        nc.vector.tensor_copy(out=xs1[:].indirect(idx[:]), in_=xe1[:])
+        junk3 = f32("junk3", 3)
+        f_pu = f32("f_pu", 1)
+        nc.scalar.activation(out=junk3[:], in_=s_sum[:], func=ACT.Copy, scale=neg_r[:], accum_out=f_pu[:])
+        junk4 = f32("junk4", 3)
+        f_p = f32("f_p", 1)
+        nc.scalar.activation(out=junk4[:], in_=k_sum[:], func=ACT.Copy, scale=neg_r[:], accum_out=f_p[:])
+        e1 = f32("e1", T)
+        d2 = f32("d2", T)
+        for cols in HALVES:
+            nc.scalar.activation(out=e1[:, cols], in_=pu[:, cols], func=ACT.Copy, scale=f_pu[:])
+            nc.gpsimd.tensor_tensor(out=d2[:, cols], in0=e1[:, cols], in1=yb[:, cols], op=ALU.add)
+        t2 = f32("t2", T)
+        for cols in HALVES:
+            nc.vector.scalar_tensor_tensor(out=t2[:, cols], in0=p[:, cols], scalar=f_p[:], in1=xs1[:, cols],
+                                           op0=ALU.mult, op1=ALU.add)
+        res = f32("res", T)
+        for h, cols in enumerate(HALVES):
+            nc.vector.tensor_tensor(out=res[:, cols], in0=t2[:, cols], in1=d2[:, cols], op=ALU.add)
+            (nc.sync, nc.scalar)[h].dma_start(out=out[:, cols], in_=res[:, cols])

@@ -62,7 +62,7 @@ def tile_attend_hvvaluepatch_kernel(tc, query, keys, gout, cvals_words, cvals_sc
         cv_scales = sb.tile([P, T], U8, name="cv_scales", align_bytes=64)
         ident = sb.tile([P, P], F32, name="ident")
         make_identity(nc, ident[:])
-        nc.gpsimd.memset(cv_scales[:].bitcast(I32), 0)
+        nc.vector.memset(cv_scales[:].bitcast(I32), 0)
         a_sb = f32("a_sb", T)
         xs1 = f32("xs1", T)
         nc.vector.memset(xs1[:], 0.0)
@@ -84,12 +84,12 @@ def tile_attend_hvvaluepatch_kernel(tc, query, keys, gout, cvals_words, cvals_sc
         nc.sync.dma_start(out=dq_raw[:], in_=dquery.rearrange("(p t) q -> p t q", t=PACK))
         go_raw = sb.tile([P, PACK, Q], F32, name="go_raw")
         nc.sync.dma_start(out=go_raw[:], in_=gout.rearrange("(p t) q -> p t q", t=PACK))
-        for g in range(4):
-            nc.gpsimd.dma_start(out=cv_scales[32 * g:32 * g + 4, :].bitcast(I32),
-                                in_=cvals_scales[0, 4 * g:4 * g + 4, :].bitcast(I32))
         corr_v = corr.rearrange("(p t) u -> t p u", t=PACK)
         planes = [sb.tile([P, U], F32, name="corr%d" % t) for t in range(PACK)]
         nc.sync.dma_start(out=planes[0][:], in_=corr_v[0])
+        for g in range(4):
+            nc.sync.dma_start(out=cv_scales[32 * g:32 * g + 4, :].bitcast(I32),
+                                in_=cvals_scales[0, 4 * g:4 * g + 4, :].bitcast(I32))
         idx2 = lists.tile([P, I // 16], U16, name="idx2")
         nc.sync.dma_start(idx2[:], offs2)
         nc.sync.dma_start(out=planes[1][:], in_=corr_v[1])
@@ -139,50 +139,46 @@ def tile_attend_hvvaluepatch_kernel(tc, query, keys, gout, cvals_words, cvals_sc
         for h, cols in enumerate(HALVES):
             nc.scalar.activation(out=p[:, cols], in_=a_sb[:, cols], func=ACT.Exp, bias=neg_max[:], accum_out=zh[:, h:h + 1])
         z = f32("z", 1)
-        nc.gpsimd.tensor_tensor(out=z[:], in0=zh[:, 0:1], in1=zh[:, 1:2], op=ALU.add)
+        nc.scalar.activation(out=z[:], in_=zh[:, 0:1], func=ACT.Identity, bias=zh[:, 1:2])
         r = f32("r", 1)
         nc.vector.reciprocal(out=r[:], in_=z[:])
-        big_r = f32("big_r", 1)
-        nc.gpsimd.tensor_scalar(out=big_r[:], in0=r[:], scalar1=OUT_SCALE, scalar2=1.0, op0=ALU.mult, op1=ALU.mult)
-        neg_r = f32("neg_r", 1)
-        nc.gpsimd.tensor_scalar(out=neg_r[:], in0=r[:], scalar1=-1.0, scalar2=1.0, op0=ALU.mult, op1=ALU.mult)
-        neg_rr = f32("neg_rr", 1)
-        nc.gpsimd.tensor_scalar(out=neg_rr[:], in0=r[:], scalar1=r[:], scalar2=-OUT_SCALE, op0=ALU.mult, op1=ALU.mult)
         ta_sb = f32("ta_sb", T)
-        picked_words = f32("picked_words", I)
-        picked = picked_words[:].bitcast(BF16).rearrange("p (t i) -> p t i", t=2)
+        xp = f32("xp", T)
         for h, cols in enumerate(HALVES):
             ta_ps = ps.tile([P, BANK], F32, name="ta_ps%d" % h)
             product(ta_ps[:], dq_codes[:], dq_scales[:], k_codes[:, cols], k_scales[:, cols])
-            nc.vector.scalar_tensor_tensor(out=picked_words[:], in0=ta_ps[:], scalar=1.0, in1=p[:, cols],
+            nc.vector.scalar_tensor_tensor(out=xp[:, cols], in0=ta_ps[:], scalar=1.0, in1=p[:, cols],
                                            op0=ALU.mult, op1=ALU.mult, accum_out=xz[:, h:h + 1])
             nc.scalar.activation(out=ta_sb[:, cols], in_=ta_ps[:], func=ACT.Copy)
-        shift = f32("shift", 1)
-        nc.gpsimd.tensor_scalar(out=shift[:], in0=xz[:, 0:1], scalar1=xz[:, 1:2], scalar2=neg_rr[:], op0=ALU.add, op1=ALU.mult)
-
         tax = sb.tile([P, T], F32, name="tax", align_bytes=64)[:, :I]
         nc.vector.tensor_copy(out=tax, in_=ta_sb[:].indirect(idx[:]))
 
-        u = f32("u", T)
-        pu = f32("pu", T)
-        for cols in HALVES:
-            nc.scalar.activation(out=u[:, cols], in_=ta_sb[:, cols], func=ACT.Identity, scale=big_r[:], bias=shift[:])
-            nc.gpsimd.tensor_tensor(out=pu[:, cols], in0=u[:, cols], in1=p[:, cols], op=ALU.mult)
+        big_r = f32("big_r", 1)
+        nc.scalar.activation(out=big_r[:], in_=r[:], func=ACT.Copy, scale=OUT_SCALE)
+        neg_r = f32("neg_r", 1)
+        nc.scalar.activation(out=neg_r[:], in_=r[:], func=ACT.Copy, scale=-1.0)
+        neg_rr = f32("neg_rr", 1)
+        nc.scalar.activation(out=neg_rr[:], in_=big_r[:], func=ACT.Copy, scale=neg_r[:])
+
+        def scaled_sum(name, parts, factor):
+            terms = f32(name + "_terms", parts.shape[1])
+            total = f32(name, 1)
+            nc.scalar.activation(out=terms[:], in_=parts, func=ACT.Copy, scale=factor[:], accum_out=total[:])
+            return total
+
+        shift = scaled_sum("shift", xz[:], neg_rr)
+        neg_mu = scaled_sum("neg_mu", xz[:], neg_r)
+
         us_ps = ps.tile([P, PACK, P], F32, name="us_ps", tag="listed")
         for t in range(PACK):
             nc.tensor.transpose(us_ps[:, t, :], us_col[:, t:t + 1].to_broadcast([P, P]), ident[:])
-        us_row = f32("us_row", I)
-        nc.scalar.activation(out=us_row[:].rearrange("q (p t) -> q p t", t=PACK),
-                             in_=us_ps[:].rearrange("q t p -> q p t"), func=ACT.Copy)
-
         px = f32("px", I)
         nc.scalar.activation(out=px[:], in_=ax[:], func=ACT.Exp, bias=neg_max[:])
         ux = f32("ux", I)
         nc.scalar.activation(out=ux[:], in_=tax, func=ACT.Identity, scale=big_r[:], bias=shift[:])
         w_val = f32("w_val", I)
-        nc.gpsimd.tensor_tensor(out=w_val[:], in0=px[:], in1=us_row[:], op=ALU.mult)
-        w_dir = f32("w_dir", I)
-        nc.gpsimd.tensor_tensor(out=w_dir[:], in0=w_val[:], in1=ux[:], op=ALU.mult)
+        nc.vector.tensor_tensor(out=w_val[:].rearrange("q (p t) -> q p t", t=PACK), in0=us_ps[:].rearrange("q t p -> q p t"),
+                                in1=px[:].rearrange("q (p t) -> q p t", t=PACK), op=ALU.mult)
 
         go_bf = sb.tile([P, Q, PACK], BF16, name="go_bf", align_bytes=64)
         go_codes = sb.tile([P, Q], U32, name="go_codes", align_bytes=64)
@@ -190,57 +186,72 @@ def tile_attend_hvvaluepatch_kernel(tc, query, keys, gout, cvals_words, cvals_sc
         weave_scalar(go_bf[:], go_raw[:])
         quantize(go_codes[:], go_scales[:], go_bf[:])
 
+        picked = sb.tile([P, 2, I], BF16, name="picked", tag="ax", align_bytes=64)
         for t in range(2):
             nc.vector.tensor_copy(out=picked[:, t, :], in_=planes[t][:].indirect(idx2[:]))
-        yb = sb.tile([P, T], F32, name="yb", tag="tax", align_bytes=64)
-        c_bf = yb[:].bitcast(BF16).rearrange("p (i t) -> p i t", t=PACK)
-        weave_scalar(c_bf[:, :, :2], picked)
+        c_bf = sb.tile([P, I, PACK], BF16, name="c_bf", tag="tax", align_bytes=64)
+        weave_scalar(c_bf[:, :, :2], picked[:])
 
-        nc.vector.tensor_copy(out=c_bf[:, :, 2], in_=planes[2][:].indirect(idx2[:]))
-
-        y = f32("y", T)
-        k_sum = f32("k_sum", 3)
+        x0 = f32("x0", T)
+        x1 = f32("x1", T)
+        k_sum = f32("k_sum", 5)
         s_sum = f32("s_sum", 3)
         c0_ps = [ps.tile([P, BANK], F32, name="c0_ps%d" % h) for h in range(2)]
         for h, cols in enumerate(HALVES):
             product(c0_ps[h][:], go_codes[:], go_scales[:], cv_words[:, cols], cv_scales[:, cols])
-            nc.vector.scalar_tensor_tensor(out=y[:, cols], in0=c0_ps[h][:], scalar=1.0, in1=pu[:, cols],
-                                           op0=ALU.mult, op1=ALU.mult, accum_out=k_sum[:, h:h + 1])
+            nc.vector.scalar_tensor_tensor(out=x0[:, cols], in0=c0_ps[h][:], scalar=1.0, in1=p[:, cols],
+                                           op0=ALU.mult, op1=ALU.mult, accum_out=s_sum[:, h:h + 1])
+            nc.scalar.activation(out=x1[:, cols], in_=x0[:, cols], func=ACT.Copy, scale=shift[:], accum_out=k_sum[:, 2 + h:3 + h])
 
-        nc.vector.tensor_copy(out=c_bf[:, :, 3], in_=planes[3][:].indirect(idx2[:]))
+        for t in range(2, PACK):
+            nc.vector.tensor_copy(out=c_bf[:, :, t], in_=planes[t][:].indirect(idx2[:]))
         c_codes = sb.tile([P, I], U32, name="c_codes", align_bytes=64)
         c_scales = sb.tile([P, I], U8, name="c_scales", align_bytes=64)
-        quantize(c_codes[:], c_scales[:], c_bf)
+        quantize(c_codes[:], c_scales[:], c_bf[:])
         c1_ps = ps.tile([P, I], F32, name="c1_ps", tag="listed")
         product(c1_ps[:], go_codes[:], go_scales[:], c_codes[:], c_scales[:])
-        xe1 = f32("xe1", I)
-        junk2 = f32("junk2", BANK)
-        nc.vector.scalar_tensor_tensor(out=junk2[:], in0=c1_ps[:], scalar=1.0, in1=w_val[:],
+        y = sb.tile([P, T], F32, name="y", tag="tax", align_bytes=64)
+        for h, cols in enumerate(HALVES):
+            nc.vector.scalar_tensor_tensor(out=y[:, cols], in0=c0_ps[h][:], scalar=big_r[:], in1=xp[:, cols],
+                                           op0=ALU.mult, op1=ALU.mult, accum_out=k_sum[:, h:h + 1])
+        hv = f32("hv", I)
+        nc.vector.scalar_tensor_tensor(out=hv[:], in0=c1_ps[:], scalar=1.0, in1=w_val[:],
                                        op0=ALU.mult, op1=ALU.mult, accum_out=s_sum[:, 2:3])
-        nc.vector.scalar_tensor_tensor(out=xe1[:], in0=c1_ps[:], scalar=1.0, in1=w_dir[:],
-                                       op0=ALU.mult, op1=ALU.mult, accum_out=k_sum[:, 2:3])
-        for h, cols in enumerate(HALVES):
-            nc.vector.scalar_tensor_tensor(out=yb[:, HALVES[1]], in0=c0_ps[h][:], scalar=1.0, in1=p[:, cols],
-                                           op0=ALU.mult, op1=ALU.mult, accum_out=s_sum[:, h:h + 1])
-        for cols in HALVES:
-            nc.gpsimd.tensor_tensor(out=yb[:, cols], in0=y[:, cols], in1=base_sb[:, cols], op=ALU.add)
+        xe1 = f32("xe1", I)
+        nc.vector.scalar_tensor_tensor(out=xe1[:], in0=hv[:], scalar=1.0, in1=ux[:],
+                                       op0=ALU.mult, op1=ALU.mult, accum_out=k_sum[:, 4:5])
         nc.vector.tensor_copy(out=xs1[:].indirect(idx[:]), in_=xe1[:])
-        junk3 = f32("junk3", 3)
-        f_pu = f32("f_pu", 1)
-        nc.scalar.activation(out=junk3[:], in_=s_sum[:], func=ACT.Copy, scale=neg_r[:], accum_out=f_pu[:])
-        junk4 = f32("junk4", 3)
+        f_xp = scaled_sum("f_xp", s_sum[:], neg_rr)
+        k_part = scaled_sum("k_part", k_sum[:], neg_r)
         f_p = f32("f_p", 1)
-        nc.scalar.activation(out=junk4[:], in_=k_sum[:], func=ACT.Copy, scale=neg_r[:], accum_out=f_p[:])
-        e1 = f32("e1", T)
-        d2 = f32("d2", T)
-        for cols in HALVES:
-            nc.scalar.activation(out=e1[:, cols], in_=pu[:, cols], func=ACT.Copy, scale=f_pu[:])
-            nc.gpsimd.tensor_tensor(out=d2[:, cols], in0=e1[:, cols], in1=yb[:, cols], op=ALU.add)
-        t2 = f32("t2", T)
-        for cols in HALVES:
-            nc.vector.scalar_tensor_tensor(out=t2[:, cols], in0=p[:, cols], scalar=f_p[:], in1=xs1[:, cols],
-                                           op0=ALU.mult, op1=ALU.add)
-        res = f32("res", T)
+        nc.scalar.activation(out=f_p[:], in_=f_xp[:], func=ACT.Identity, scale=neg_mu[:], bias=k_part[:])
+
+        fixed_t = f32("fixed_t", T)
+        fixed_ps = []
         for h, cols in enumerate(HALVES):
-            nc.vector.tensor_tensor(out=res[:, cols], in0=t2[:, cols], in1=d2[:, cols], op=ALU.add)
+            turned = ps.tile([P, BANK], F32, name="turned%d" % h, tag="a_ps%d" % h)
+            for b in range(BANK // P):
+                block = slice(cols.start + b * P, cols.start + (b + 1) * P)
+                for n, term in enumerate((y, x1, base_sb)):
+                    nc.tensor.matmul(turned[:, b * P:(b + 1) * P], term[:, block], ident[:],
+                                     start=(n == 0), stop=(n == 2), is_transpose=True)
+            nc.scalar.activation(out=fixed_t[:, cols], in_=turned[:], func=ACT.Copy)
+        for h, cols in enumerate(HALVES):
+            back = ps.tile([P, BANK], F32, name="back%d" % h, tag="ta_ps%d" % h)
+            for b in range(BANK // P):
+                block = slice(cols.start + b * P, cols.start + (b + 1) * P)
+                nc.tensor.transpose(back[:, b * P:(b + 1) * P], fixed_t[:, block], ident[:])
+            fixed_ps.append(back)
+
+        t1 = f32("t1", T)
+        t2 = f32("t2", T)
+        res = f32("res", T)
+        for cols in HALVES:
+            nc.vector.scalar_tensor_tensor(out=t1[:, cols], in0=p[:, cols], scalar=f_p[:], in1=xs1[:, cols],
+                                           op0=ALU.mult, op1=ALU.add)
+        for cols in HALVES:
+            nc.vector.scalar_tensor_tensor(out=t2[:, cols], in0=xp[:, cols], scalar=f_xp[:], in1=t1[:, cols],
+                                           op0=ALU.mult, op1=ALU.add)
+        for h, cols in enumerate(HALVES):
+            nc.vector.tensor_tensor(out=res[:, cols], in0=fixed_ps[h][:], in1=t2[:, cols], op=ALU.add)
             (nc.sync, nc.scalar)[h].dma_start(out=out[:, cols], in_=res[:, cols])

@@ -21,8 +21,8 @@ P = 128
 PACK = 4
 BANK = 512
 OUT_SCALE = 1024.0
-KEY_CHUNK = 256
-KEY_CHUNKS = tuple((c0, KEY_CHUNK) for c0 in range(0, T, KEY_CHUNK))
+KEY_CHUNKS = ((0, 256, 128), (256, 512, 320), (768, 256, 96))
+STORE_PIECES = ((0, 512), (512, 256), (768, 256))
 HALVES = (slice(0, BANK), slice(BANK, T))
 
 
@@ -71,7 +71,7 @@ def tile_attend_hvvaluepatch_kernel(tc, query, keys, gout, cvals_words, cvals_sc
         nc.sync.dma_start(out=q_raw[:], in_=query.rearrange("(p t) q -> p t q", t=PACK))
         keys_v = keys.rearrange("(p t) n -> p t n", t=PACK)
         k_raw = []
-        for c, (c0, w) in enumerate(KEY_CHUNKS):
+        for c, (c0, w, wv) in enumerate(KEY_CHUNKS):
             kt = sb.tile([P, PACK, w], F32, name="k_raw%d" % c)
             nc.sync.dma_start(out=kt[:], in_=keys_v[:, :, c0:c0 + w])
             k_raw.append(kt)
@@ -87,15 +87,15 @@ def tile_attend_hvvaluepatch_kernel(tc, query, keys, gout, cvals_words, cvals_sc
         corr_v = corr.rearrange("(p t) u -> t p u", t=PACK)
         planes = [sb.tile([P, U], F32, name="corr%d" % t) for t in range(PACK)]
         nc.sync.dma_start(out=planes[0][:], in_=corr_v[0])
-        for g in range(4):
-            nc.sync.dma_start(out=cv_scales[32 * g:32 * g + 4, :].bitcast(I32),
-                                in_=cvals_scales[0, 4 * g:4 * g + 4, :].bitcast(I32))
         idx2 = lists.tile([P, I // 16], U16, name="idx2")
         nc.sync.dma_start(idx2[:], offs2)
         nc.sync.dma_start(out=planes[1][:], in_=corr_v[1])
         cv_words = sb.tile([P, T], U32, name="cv_words", align_bytes=64)
         nc.sync.dma_start(out=cv_words[:].bitcast(I32),
                           in_=cvals_words[0].rearrange("p n t -> p (n t)").bitcast(I32))
+        for g in range(4):
+            nc.sync.dma_start(out=cv_scales[32 * g:32 * g + 4, :].bitcast(I32),
+                                in_=cvals_scales[0, 4 * g:4 * g + 4, :].bitcast(I32))
         nc.sync.dma_start(out=planes[2][:], in_=corr_v[2])
         nc.sync.dma_start(out=planes[3][:], in_=corr_v[3])
         base_sb = f32("base_sb", T)
@@ -110,19 +110,12 @@ def tile_attend_hvvaluepatch_kernel(tc, query, keys, gout, cvals_words, cvals_sc
         k_codes = sb.tile([P, T], U32, name="k_codes", align_bytes=64)
         k_scales = sb.tile([P, T], U8, name="k_scales", align_bytes=64)
         row_max = None
-        for c, (c0, w) in enumerate(KEY_CHUNKS):
-            wv = w * 5 // 8 if c == len(KEY_CHUNKS) - 1 else w * 3 // 8
+        for c, (c0, w, wv) in enumerate(KEY_CHUNKS):
             weave_vector(k_bf[:, c0:c0 + wv, :], k_raw[c][:, :, :wv])
             weave_scalar(k_bf[:, c0 + wv:c0 + w, :], k_raw[c][:, :, wv:])
             quantize(k_codes[:, c0:c0 + w], k_scales[:, c0:c0 + w], k_bf[:, c0:c0 + w, :])
             a_ps = ps.tile([P, w], F32, name="a_ps%d" % c, tag="a_ps%d" % (c % 2))
             product(a_ps[:], q_codes[:], q_scales[:], k_codes[:, c0:c0 + w], k_scales[:, c0:c0 + w])
-            if c == len(KEY_CHUNKS) - 1:
-                dq_bf = sb.tile([P, Q, PACK], BF16, name="dq_bf", align_bytes=64)
-                dq_codes = sb.tile([P, Q], U32, name="dq_codes", align_bytes=64)
-                dq_scales = sb.tile([P, Q], U8, name="dq_scales", align_bytes=64)
-                weave_scalar(dq_bf[:], dq_raw[:])
-                quantize(dq_codes[:], dq_scales[:], dq_bf[:])
             new_max = f32("row_max%d" % c, 1)
             nc.vector.tensor_scalar(out=a_sb[:, c0:c0 + w], in0=a_ps[:], scalar1=0.0,
                                     scalar2=None if row_max is None else row_max[:],
@@ -133,9 +126,13 @@ def tile_attend_hvvaluepatch_kernel(tc, query, keys, gout, cvals_words, cvals_sc
 
         ax = f32("ax", I)
         nc.vector.tensor_copy(out=ax[:], in_=a_sb[:].indirect(idx[:]))
+        dq_bf = sb.tile([P, Q, PACK], BF16, name="dq_bf", align_bytes=64)
+        dq_codes = sb.tile([P, Q], U32, name="dq_codes", align_bytes=64)
+        dq_scales = sb.tile([P, Q], U8, name="dq_scales", align_bytes=64)
+        weave_scalar(dq_bf[:], dq_raw[:])
+        quantize(dq_codes[:], dq_scales[:], dq_bf[:])
         p = f32("p", T)
         zh = f32("zh", 2)
-        xz = f32("xz", 2)
         for h, cols in enumerate(HALVES):
             nc.scalar.activation(out=p[:, cols], in_=a_sb[:, cols], func=ACT.Exp, bias=neg_max[:], accum_out=zh[:, h:h + 1])
         z = f32("z", 1)
@@ -147,18 +144,17 @@ def tile_attend_hvvaluepatch_kernel(tc, query, keys, gout, cvals_words, cvals_sc
         for h, cols in enumerate(HALVES):
             ta_ps = ps.tile([P, BANK], F32, name="ta_ps%d" % h)
             product(ta_ps[:], dq_codes[:], dq_scales[:], k_codes[:, cols], k_scales[:, cols])
-            nc.vector.scalar_tensor_tensor(out=xp[:, cols], in0=ta_ps[:], scalar=1.0, in1=p[:, cols],
-                                           op0=ALU.mult, op1=ALU.mult, accum_out=xz[:, h:h + 1])
             nc.scalar.activation(out=ta_sb[:, cols], in_=ta_ps[:], func=ACT.Copy)
-        tax = sb.tile([P, T], F32, name="tax", align_bytes=64)[:, :I]
-        nc.vector.tensor_copy(out=tax, in_=ta_sb[:].indirect(idx[:]))
+            nc.gpsimd.tensor_tensor(out=xp[:, cols], in0=ta_sb[:, cols], in1=p[:, cols], op=ALU.mult)
+        tax = f32("tax", I)
+        nc.vector.tensor_copy(out=tax[:], in_=ta_sb[:].indirect(idx[:]))
 
+        px = f32("px", I)
+        nc.scalar.activation(out=px[:], in_=ax[:], func=ACT.Exp, bias=neg_max[:])
         big_r = f32("big_r", 1)
         nc.scalar.activation(out=big_r[:], in_=r[:], func=ACT.Copy, scale=OUT_SCALE)
         neg_r = f32("neg_r", 1)
         nc.scalar.activation(out=neg_r[:], in_=r[:], func=ACT.Copy, scale=-1.0)
-        neg_rr = f32("neg_rr", 1)
-        nc.scalar.activation(out=neg_rr[:], in_=big_r[:], func=ACT.Copy, scale=neg_r[:])
 
         def scaled_sum(name, parts, factor):
             terms = f32(name + "_terms", parts.shape[1])
@@ -166,19 +162,22 @@ def tile_attend_hvvaluepatch_kernel(tc, query, keys, gout, cvals_words, cvals_sc
             nc.scalar.activation(out=terms[:], in_=parts, func=ACT.Copy, scale=factor[:], accum_out=total[:])
             return total
 
-        shift = scaled_sum("shift", xz[:], neg_rr)
-        neg_mu = scaled_sum("neg_mu", xz[:], neg_r)
+        xpr = f32("xpr", T)
+        xzr = f32("xzr", 1)
+        nc.scalar.activation(out=xpr[:], in_=xp[:], func=ACT.Copy, scale=big_r[:], accum_out=xzr[:])
+        neg_mu = f32("neg_mu", 1)
+        nc.scalar.activation(out=neg_mu[:], in_=xzr[:], func=ACT.Copy, scale=-1.0 / OUT_SCALE)
 
         us_ps = ps.tile([P, PACK, P], F32, name="us_ps", tag="listed")
         for t in range(PACK):
             nc.tensor.transpose(us_ps[:, t, :], us_col[:, t:t + 1].to_broadcast([P, P]), ident[:])
-        px = f32("px", I)
-        nc.scalar.activation(out=px[:], in_=ax[:], func=ACT.Exp, bias=neg_max[:])
+        us_row = f32("us_row", I)
+        nc.scalar.activation(out=us_row[:].rearrange("q (p t) -> q p t", t=PACK),
+                             in_=us_ps[:].rearrange("q t p -> q p t"), func=ACT.Copy)
         ux = f32("ux", I)
-        nc.scalar.activation(out=ux[:], in_=tax, func=ACT.Identity, scale=big_r[:], bias=shift[:])
+        nc.scalar.activation(out=ux[:], in_=tax[:], func=ACT.Identity, scale=-OUT_SCALE, bias=xzr[:])
         w_val = f32("w_val", I)
-        nc.vector.tensor_tensor(out=w_val[:].rearrange("q (p t) -> q p t", t=PACK), in0=us_ps[:].rearrange("q t p -> q p t"),
-                                in1=px[:].rearrange("q (p t) -> q p t", t=PACK), op=ALU.mult)
+        nc.gpsimd.tensor_tensor(out=w_val[:], in0=px[:], in1=us_row[:], op=ALU.mult)
 
         go_bf = sb.tile([P, Q, PACK], BF16, name="go_bf", align_bytes=64)
         go_codes = sb.tile([P, Q], U32, name="go_codes", align_bytes=64)
@@ -186,22 +185,22 @@ def tile_attend_hvvaluepatch_kernel(tc, query, keys, gout, cvals_words, cvals_sc
         weave_scalar(go_bf[:], go_raw[:])
         quantize(go_codes[:], go_scales[:], go_bf[:])
 
-        picked = sb.tile([P, 2, I], BF16, name="picked", tag="ax", align_bytes=64)
+        picked = sb.tile([P, 2, I], BF16, name="picked", align_bytes=64)
         for t in range(2):
             nc.vector.tensor_copy(out=picked[:, t, :], in_=planes[t][:].indirect(idx2[:]))
-        c_bf = sb.tile([P, I, PACK], BF16, name="c_bf", tag="tax", align_bytes=64)
+        c_bf = sb.tile([P, I, PACK], BF16, name="c_bf", align_bytes=64)
         weave_scalar(c_bf[:, :, :2], picked[:])
 
-        x0 = f32("x0", T)
         x1 = f32("x1", T)
+        x2 = f32("x2", T)
         k_sum = f32("k_sum", 5)
         s_sum = f32("s_sum", 3)
         c0_ps = [ps.tile([P, BANK], F32, name="c0_ps%d" % h) for h in range(2)]
         for h, cols in enumerate(HALVES):
             product(c0_ps[h][:], go_codes[:], go_scales[:], cv_words[:, cols], cv_scales[:, cols])
-            nc.vector.scalar_tensor_tensor(out=x0[:, cols], in0=c0_ps[h][:], scalar=1.0, in1=p[:, cols],
+            nc.vector.scalar_tensor_tensor(out=x1[:, cols], in0=c0_ps[h][:], scalar=neg_r[:], in1=p[:, cols],
                                            op0=ALU.mult, op1=ALU.mult, accum_out=s_sum[:, h:h + 1])
-            nc.scalar.activation(out=x1[:, cols], in_=x0[:, cols], func=ACT.Copy, scale=shift[:], accum_out=k_sum[:, 2 + h:3 + h])
+            nc.scalar.activation(out=x2[:, cols], in_=x1[:, cols], func=ACT.Copy, scale=xzr[:], accum_out=k_sum[:, 2 + h:3 + h])
 
         for t in range(2, PACK):
             nc.vector.tensor_copy(out=c_bf[:, :, t], in_=planes[t][:].indirect(idx2[:]))
@@ -210,30 +209,36 @@ def tile_attend_hvvaluepatch_kernel(tc, query, keys, gout, cvals_words, cvals_sc
         quantize(c_codes[:], c_scales[:], c_bf[:])
         c1_ps = ps.tile([P, I], F32, name="c1_ps", tag="listed")
         product(c1_ps[:], go_codes[:], go_scales[:], c_codes[:], c_scales[:])
-        y = sb.tile([P, T], F32, name="y", tag="tax", align_bytes=64)
+        y = sb.tile([P, T], F32, name="y", tag="c_bf", align_bytes=64)
         for h, cols in enumerate(HALVES):
-            nc.vector.scalar_tensor_tensor(out=y[:, cols], in0=c0_ps[h][:], scalar=big_r[:], in1=xp[:, cols],
+            nc.vector.scalar_tensor_tensor(out=y[:, cols], in0=c0_ps[h][:], scalar=1.0, in1=xpr[:, cols],
                                            op0=ALU.mult, op1=ALU.mult, accum_out=k_sum[:, h:h + 1])
         hv = f32("hv", I)
-        nc.vector.scalar_tensor_tensor(out=hv[:], in0=c1_ps[:], scalar=1.0, in1=w_val[:],
+        nc.vector.scalar_tensor_tensor(out=hv[:], in0=c1_ps[:], scalar=neg_r[:], in1=w_val[:],
                                        op0=ALU.mult, op1=ALU.mult, accum_out=s_sum[:, 2:3])
         xe1 = f32("xe1", I)
         nc.vector.scalar_tensor_tensor(out=xe1[:], in0=hv[:], scalar=1.0, in1=ux[:],
                                        op0=ALU.mult, op1=ALU.mult, accum_out=k_sum[:, 4:5])
         nc.vector.tensor_copy(out=xs1[:].indirect(idx[:]), in_=xe1[:])
-        f_xp = scaled_sum("f_xp", s_sum[:], neg_rr)
+        f_xp = scaled_sum("f_xp", s_sum[:], big_r)
         k_part = scaled_sum("k_part", k_sum[:], neg_r)
         f_p = f32("f_p", 1)
         nc.scalar.activation(out=f_p[:], in_=f_xp[:], func=ACT.Identity, scale=neg_mu[:], bias=k_part[:])
+        e = f32("e", T)
+        pe = f32("pe", T)
+        for cols in HALVES:
+            nc.scalar.activation(out=e[:, cols], in_=ta_sb[:, cols], func=ACT.Identity, scale=f_xp[:], bias=f_p[:])
+            nc.gpsimd.tensor_tensor(out=pe[:, cols], in0=e[:, cols], in1=p[:, cols], op=ALU.mult)
 
         fixed_t = f32("fixed_t", T)
         fixed_ps = []
         for h, cols in enumerate(HALVES):
             turned = ps.tile([P, BANK], F32, name="turned%d" % h, tag="a_ps%d" % h)
             for b in range(BANK // P):
+                local = slice(b * P, (b + 1) * P)
                 block = slice(cols.start + b * P, cols.start + (b + 1) * P)
-                for n, term in enumerate((y, x1, base_sb)):
-                    nc.tensor.matmul(turned[:, b * P:(b + 1) * P], term[:, block], ident[:],
+                for n, term in enumerate((y[:, block], x2[:, block], base_sb[:, block])):
+                    nc.tensor.matmul(turned[:, local], term, ident[:],
                                      start=(n == 0), stop=(n == 2), is_transpose=True)
             nc.scalar.activation(out=fixed_t[:, cols], in_=turned[:], func=ACT.Copy)
         for h, cols in enumerate(HALVES):
@@ -244,14 +249,10 @@ def tile_attend_hvvaluepatch_kernel(tc, query, keys, gout, cvals_words, cvals_sc
             fixed_ps.append(back)
 
         t1 = f32("t1", T)
-        t2 = f32("t2", T)
         res = f32("res", T)
-        for cols in HALVES:
-            nc.vector.scalar_tensor_tensor(out=t1[:, cols], in0=p[:, cols], scalar=f_p[:], in1=xs1[:, cols],
-                                           op0=ALU.mult, op1=ALU.add)
-        for cols in HALVES:
-            nc.vector.scalar_tensor_tensor(out=t2[:, cols], in0=xp[:, cols], scalar=f_xp[:], in1=t1[:, cols],
-                                           op0=ALU.mult, op1=ALU.add)
         for h, cols in enumerate(HALVES):
-            nc.vector.tensor_tensor(out=res[:, cols], in0=fixed_ps[h][:], in1=t2[:, cols], op=ALU.add)
-            (nc.sync, nc.scalar)[h].dma_start(out=out[:, cols], in_=res[:, cols])
+            nc.vector.tensor_tensor(out=t1[:, cols], in0=fixed_ps[h][:], in1=xs1[:, cols], op=ALU.add)
+        for n, (c0, w) in enumerate(STORE_PIECES):
+            cols = slice(c0, c0 + w)
+            nc.vector.tensor_tensor(out=res[:, cols], in0=t1[:, cols], in1=pe[:, cols], op=ALU.add)
+            (nc.sync, nc.scalar)[n % 2].dma_start(out=out[:, cols], in_=res[:, cols])

@@ -124,13 +124,13 @@ def tile_attend_hvvaluepatch_kernel(tc, query, keys, gout, cvals_words, cvals_sc
         neg_max = f32("neg_max", 1)
         nc.scalar.activation(out=neg_max[:], in_=row_max[:], func=ACT.Copy, scale=-1.0)
 
-        ax = f32("ax", I)
-        nc.vector.tensor_copy(out=ax[:], in_=a_sb[:].indirect(idx[:]))
         dq_bf = sb.tile([P, Q, PACK], BF16, name="dq_bf", align_bytes=64)
         dq_codes = sb.tile([P, Q], U32, name="dq_codes", align_bytes=64)
         dq_scales = sb.tile([P, Q], U8, name="dq_scales", align_bytes=64)
         weave_scalar(dq_bf[:], dq_raw[:])
         quantize(dq_codes[:], dq_scales[:], dq_bf[:])
+        ax = sb.tile([P, I], F32, name="ax", tag="dq_bf", align_bytes=64)
+        nc.vector.tensor_copy(out=ax[:], in_=a_sb[:].indirect(idx[:]))
         p = f32("p", T)
         zh = f32("zh", 2)
         for h, cols in enumerate(HALVES):
@@ -175,9 +175,11 @@ def tile_attend_hvvaluepatch_kernel(tc, query, keys, gout, cvals_words, cvals_sc
         nc.scalar.activation(out=us_row[:].rearrange("q (p t) -> q p t", t=PACK),
                              in_=us_ps[:].rearrange("q t p -> q p t"), func=ACT.Copy)
         ux = f32("ux", I)
-        nc.scalar.activation(out=ux[:], in_=tax[:], func=ACT.Identity, scale=-OUT_SCALE, bias=xzr[:])
         w_val = f32("w_val", I)
         nc.gpsimd.tensor_tensor(out=w_val[:], in0=px[:], in1=us_row[:], op=ALU.mult)
+        nc.gpsimd.tensor_scalar(out=ux[:], in0=tax[:], scalar1=-OUT_SCALE, scalar2=xzr[:], op0=ALU.mult, op1=ALU.add)
+        w_dir = f32("w_dir", I)
+        nc.gpsimd.tensor_tensor(out=w_dir[:], in0=w_val[:], in1=ux[:], op=ALU.mult)
 
         go_bf = sb.tile([P, Q, PACK], BF16, name="go_bf", align_bytes=64)
         go_codes = sb.tile([P, Q], U32, name="go_codes", align_bytes=64)
@@ -198,8 +200,15 @@ def tile_attend_hvvaluepatch_kernel(tc, query, keys, gout, cvals_words, cvals_sc
         c0_ps = [ps.tile([P, BANK], F32, name="c0_ps%d" % h) for h in range(2)]
         for h, cols in enumerate(HALVES):
             product(c0_ps[h][:], go_codes[:], go_scales[:], cv_words[:, cols], cv_scales[:, cols])
-            nc.vector.scalar_tensor_tensor(out=x1[:, cols], in0=c0_ps[h][:], scalar=neg_r[:], in1=p[:, cols],
-                                           op0=ALU.mult, op1=ALU.mult, accum_out=s_sum[:, h:h + 1])
+            if h == 0:
+                c0_sb = f32("c0_sb", BANK)
+                x0 = f32("x0", BANK)
+                nc.scalar.activation(out=c0_sb[:], in_=c0_ps[h][:], func=ACT.Copy)
+                nc.gpsimd.tensor_tensor(out=x0[:], in0=c0_sb[:], in1=p[:, cols], op=ALU.mult)
+                nc.scalar.activation(out=x1[:, cols], in_=x0[:], func=ACT.Copy, scale=neg_r[:], accum_out=s_sum[:, h:h + 1])
+            else:
+                nc.vector.scalar_tensor_tensor(out=x1[:, cols], in0=c0_ps[h][:], scalar=neg_r[:], in1=p[:, cols],
+                                               op0=ALU.mult, op1=ALU.mult, accum_out=s_sum[:, h:h + 1])
             nc.scalar.activation(out=x2[:, cols], in_=x1[:, cols], func=ACT.Copy, scale=xzr[:], accum_out=k_sum[:, 2 + h:3 + h])
 
         for t in range(2, PACK):
@@ -213,15 +222,15 @@ def tile_attend_hvvaluepatch_kernel(tc, query, keys, gout, cvals_words, cvals_sc
         for h, cols in enumerate(HALVES):
             nc.vector.scalar_tensor_tensor(out=y[:, cols], in0=c0_ps[h][:], scalar=1.0, in1=xpr[:, cols],
                                            op0=ALU.mult, op1=ALU.mult, accum_out=k_sum[:, h:h + 1])
+        xe1 = f32("xe1", I)
+        nc.vector.scalar_tensor_tensor(out=xe1[:], in0=c1_ps[:], scalar=neg_r[:], in1=w_dir[:],
+                                       op0=ALU.mult, op1=ALU.mult, accum_out=k_sum[:, 4:5])
         hv = f32("hv", I)
         nc.vector.scalar_tensor_tensor(out=hv[:], in0=c1_ps[:], scalar=neg_r[:], in1=w_val[:],
                                        op0=ALU.mult, op1=ALU.mult, accum_out=s_sum[:, 2:3])
-        xe1 = f32("xe1", I)
-        nc.vector.scalar_tensor_tensor(out=xe1[:], in0=hv[:], scalar=1.0, in1=ux[:],
-                                       op0=ALU.mult, op1=ALU.mult, accum_out=k_sum[:, 4:5])
         nc.vector.tensor_copy(out=xs1[:].indirect(idx[:]), in_=xe1[:])
-        f_xp = scaled_sum("f_xp", s_sum[:], big_r)
         k_part = scaled_sum("k_part", k_sum[:], neg_r)
+        f_xp = scaled_sum("f_xp", s_sum[:], big_r)
         f_p = f32("f_p", 1)
         nc.scalar.activation(out=f_p[:], in_=f_xp[:], func=ACT.Identity, scale=neg_mu[:], bias=k_part[:])
         e = f32("e", T)

from contextlib import ExitStack

import concourse.mybir as mybir
from concourse.masks import make_identity

D, E, T, I, U, Q = 512, 512, 1024, 512, 2048, 128
FLOPS = 2 * Q * (2 * D * T + E * T + E * I)

F32 = mybir.dt.float32
BF16 = mybir.dt.bfloat16
I32 = mybir.dt.int32
U32 = mybir.dt.uint32
U16 = mybir.dt.uint16
U8 = mybir.dt.uint8
FP8X4 = mybir.dt.float8_e4m3fn_x4
ALU = mybir.AluOpType
ACT = mybir.ActivationFunctionType
AXIS = mybir.AxisListType

P = 128
PACK = 4
BANK = 512
OUT_SCALE = 1024.0
KEY_CHUNKS = ((0, 256, 128), (256, 512, 320), (768, 256, 96))
STORE_PIECES = ((0, 512), (512, 256), (768, 256))
HALVES = (slice(0, BANK), slice(BANK, T))


def tile_attend_hvvaluepatch_kernel(tc, query, keys, gout, cvals_words, cvals_scales, corr, us, dquery, base, offs, offs2, out):
    nc = tc.nc

    def weave_views(dst, src):
        return (dst.rearrange("p (c i) t -> p c t i", i=4), src.rearrange("p t (c i) -> p c t i", i=4))

    def weave_vector(dst, src):
        d, s = weave_views(dst, src)
        nc.vector.tensor_copy(out=d, in_=s)

    def weave_scalar(dst, src):
        d, s = weave_views(dst, src)
        nc.scalar.activation(out=d, in_=s, func=ACT.Copy)

    def quantize(codes, scales, woven):
        nc.vector.quantize_mx(out=codes.bitcast(FP8X4), scales=scales, in_=woven.rearrange("p w t -> p (w t)"))

    def product(bank, l_codes, l_scales, r_codes, r_scales):
        nc.tensor.matmul_mx(out=bank, lhsT=l_codes.bitcast(FP8X4), lhsT_scale=l_scales,
                            rhs=r_codes.bitcast(FP8X4), rhs_scale=r_scales, start=True, stop=True)

    with ExitStack() as ctx:
        lists = ctx.enter_context(tc.tile_pool(name="lists", bufs=1))
        sb = ctx.enter_context(tc.tile_pool(name="sb", bufs=1))
        ps = ctx.enter_context(tc.psum_pool(name="ps", bufs=1))

        def f32(name, width):
            return sb.tile([P, width], F32, name=name, align_bytes=64)

        warm = f32("warm", 1)
        nc.vector.memset(warm[:], 0.0)
        warm_out = f32("warm_out", 1)
        nc.scalar.activation(out=warm_out[:], in_=warm[:], func=ACT.Exp)
        cv_scales = sb.tile([P, T], U8, name="cv_scales", align_bytes=64)
        ident = sb.tile([P, P], F32, name="ident")
        make_identity(nc, ident[:])
        nc.vector.memset(cv_scales[:].bitcast(I32), 0)
        a_sb = f32("a_sb", T)
        xs1 = f32("xs1", T)
        nc.vector.memset(xs1[:], 0.0)

        q_raw = sb.tile([P, PACK, Q], F32, name="q_raw")
        nc.sync.dma_start(out=q_raw[:], in_=query.rearrange("(p t) q -> p t q", t=PACK))
        keys_v = keys.rearrange("(p t) n -> p t n", t=PACK)
        k_raw = []
        for c, (c0, w, wv) in enumerate(KEY_CHUNKS):
            kt = sb.tile([P, PACK, w], F32, name="k_raw%d" % c)
            nc.sync.dma_start(out=kt[:], in_=keys_v[:, :, c0:c0 + w])
            k_raw.append(kt)
            if c == 0:
                us_col = sb.tile([P, PACK], F32, name="us_col")
                nc.sync.dma_start(out=us_col[:], in_=us.rearrange("o (p t) -> (o p) t", t=PACK))
                idx = lists.tile([P, I // 16], U16, name="idx")
                nc.sync.dma_start(idx[:], offs)
        dq_raw = sb.tile([P, PACK, Q], F32, name="dq_raw")
        nc.sync.dma_start(out=dq_raw[:], in_=dquery.rearrange("(p t) q -> p t q", t=PACK))
        go_raw = sb.tile([P, PACK, Q], F32, name="go_raw")
        nc.sync.dma_start(out=go_raw[:], in_=gout.rearrange("(p t) q -> p t q", t=PACK))
        corr_v = corr.rearrange("(p t) u -> t p u", t=PACK)
        planes = [sb.tile([P, U], F32, name="corr%d" % t) for t in range(PACK)]
        nc.sync.dma_start(out=planes[0][:], in_=corr_v[0])
        idx2 = lists.tile([P, I // 16], U16, name="idx2")
        nc.sync.dma_start(idx2[:], offs2)
        nc.sync.dma_start(out=planes[1][:], in_=corr_v[1])
        cv_words = sb.tile([P, T], U32, name="cv_words", align_bytes=64)
        nc.sync.dma_start(out=cv_words[:].bitcast(I32),
                          in_=cvals_words[0].rearrange("p n t -> p (n t)").bitcast(I32))
        for g in range(4):
            nc.sync.dma_start(out=cv_scales[32 * g:32 * g + 4, :].bitcast(I32),
                                in_=cvals_scales[0, 4 * g:4 * g + 4, :].bitcast(I32))
        nc.sync.dma_start(out=planes[2][:], in_=corr_v[2])
        nc.sync.dma_start(out=planes[3][:], in_=corr_v[3])
        base_sb = f32("base_sb", T)
        nc.sync.dma_start(out=base_sb[:], in_=base)

        q_bf = sb.tile([P, Q, PACK], BF16, name="q_bf", align_bytes=64)
        q_codes = sb.tile([P, Q], U32, name="q_codes", align_bytes=64)
        q_scales = sb.tile([P, Q], U8, name="q_scales", align_bytes=64)
        weave_vector(q_bf[:], q_raw[:])
        quantize(q_codes[:], q_scales[:], q_bf[:])
        k_bf = sb.tile([P, T, PACK], BF16, name="k_bf", align_bytes=64)
        k_codes = sb.tile([P, T], U32, name="k_codes", align_bytes=64)
        k_scales = sb.tile([P, T], U8, name="k_scales", align_bytes=64)
        row_max = None
        for c, (c0, w, wv) in enumerate(KEY_CHUNKS):
            weave_vector(k_bf[:, c0:c0 + wv, :], k_raw[c][:, :, :wv])
            weave_scalar(k_bf[:, c0 + wv:c0 + w, :], k_raw[c][:, :, wv:])
            quantize(k_codes[:, c0:c0 + w], k_scales[:, c0:c0 + w], k_bf[:, c0:c0 + w, :])
            a_ps = ps.tile([P, w], F32, name="a_ps%d" % c, tag="a_ps%d" % (c % 2))
            product(a_ps[:], q_codes[:], q_scales[:], k_codes[:, c0:c0 + w], k_scales[:, c0:c0 + w])
            new_max = f32("row_max%d" % c, 1)
            nc.vector.tensor_scalar(out=a_sb[:, c0:c0 + w], in0=a_ps[:], scalar1=0.0,
                                    scalar2=None if row_max is None else row_max[:],
                                    op0=ALU.add, op1=ALU.max, accum_out=new_max[:])
            row_max = new_max
        neg_max = f32("neg_max", 1)
        nc.scalar.activation(out=neg_max[:], in_=row_max[:], func=ACT.Copy, scale=-1.0)

        dq_bf = sb.tile([P, Q, PACK], BF16, name="dq_bf", align_bytes=64)
        dq_codes = sb.tile([P, Q], U32, name="dq_codes", align_bytes=64)
        dq_scales = sb.tile([P, Q], U8, name="dq_scales", align_bytes=64)
        weave_scalar(dq_bf[:], dq_raw[:])
        quantize(dq_codes[:], dq_scales[:], dq_bf[:])
        ax = sb.tile([P, I], F32, name="ax", tag="dq_bf", align_bytes=64)
        nc.vector.tensor_copy(out=ax[:], in_=a_sb[:].indirect(idx[:]))
        p = f32("p", T)
        zh = f32("zh", 2)
        for h, cols in enumerate(HALVES):
            nc.scalar.activation(out=p[:, cols], in_=a_sb[:, cols], func=ACT.Exp, bias=neg_max[:], accum_out=zh[:, h:h + 1])
        z = f32("z", 1)
        nc.scalar.activation(out=z[:], in_=zh[:, 0:1], func=ACT.Identity, bias=zh[:, 1:2])
        r = f32("r", 1)
        nc.vector.reciprocal(out=r[:], in_=z[:])
        ta_sb = f32("ta_sb", T)
        xp = f32("xp", T)
        for h, cols in enumerate(HALVES):
            ta_ps = ps.tile([P, BANK], F32, name="ta_ps%d" % h)
            product(ta_ps[:], dq_codes[:], dq_scales[:], k_codes[:, cols], k_scales[:, cols])
            nc.scalar.activation(out=ta_sb[:, cols], in_=ta_ps[:], func=ACT.Copy)
            nc.gpsimd.tensor_tensor(out=xp[:, cols], in0=ta_sb[:, cols], in1=p[:, cols], op=ALU.mult)
        tax = f32("tax", I)
        nc.vector.tensor_copy(out=tax[:], in_=ta_sb[:].indirect(idx[:]))

        px = f32("px", I)
        nc.scalar.activation(out=px[:], in_=ax[:], func=ACT.Exp, bias=neg_max[:])
        big_r = f32("big_r", 1)
        nc.scalar.activation(out=big_r[:], in_=r[:], func=ACT.Copy, scale=OUT_SCALE)
        neg_r = f32("neg_r", 1)
        nc.scalar.activation(out=neg_r[:], in_=r[:], func=ACT.Copy, scale=-1.0)

        def scaled_sum(name, parts, factor):
            terms = f32(name + "_terms", parts.shape[1])
            total = f32(name, 1)
            nc.scalar.activation(out=terms[:], in_=parts, func=ACT.Copy, scale=factor[:], accum_out=total[:])
            return total

        xpr = f32("xpr", T)
        xzr = f32("xzr", 1)
        nc.scalar.activation(out=xpr[:], in_=xp[:], func=ACT.Copy, scale=big_r[:], accum_out=xzr[:])
        neg_mu = f32("neg_mu", 1)
        nc.scalar.activation(out=neg_mu[:], in_=xzr[:], func=ACT.Copy, scale=-1.0 / OUT_SCALE)

        us_ps = ps.tile([P, PACK, P], F32, name="us_ps", tag="listed")
        for t in range(PACK):
            nc.tensor.transpose(us_ps[:, t, :], us_col[:, t:t + 1].to_broadcast([P, P]), ident[:])
        us_row = f32("us_row", I)
        nc.scalar.activation(out=us_row[:].rearrange("q (p t) -> q p t", t=PACK),
                             in_=us_ps[:].rearrange("q t p -> q p t"), func=ACT.Copy)
        ux = f32("ux", I)
        w_val = f32("w_val", I)
        nc.gpsimd.tensor_tensor(out=w_val[:], in0=px[:], in1=us_row[:], op=ALU.mult)
        nc.gpsimd.tensor_scalar(out=ux[:], in0=tax[:], scalar1=-OUT_SCALE, scalar2=xzr[:], op0=ALU.mult, op1=ALU.add)
        w_dir = f32("w_dir", I)
        nc.gpsimd.tensor_tensor(out=w_dir[:], in0=w_val[:], in1=ux[:], op=ALU.mult)

        go_bf = sb.tile([P, Q, PACK], BF16, name="go_bf", align_bytes=64)
        go_codes = sb.tile([P, Q], U32, name="go_codes", align_bytes=64)
        go_scales = sb.tile([P, Q], U8, name="go_scales", align_bytes=64)
        weave_scalar(go_bf[:], go_raw[:])
        quantize(go_codes[:], go_scales[:], go_bf[:])

        picked = sb.tile([P, 2, I], BF16, name="picked", align_bytes=64)
        for t in range(2):
            nc.vector.tensor_copy(out=picked[:, t, :], in_=planes[t][:].indirect(idx2[:]))
        c_bf = sb.tile([P, I, PACK], BF16, name="c_bf", align_bytes=64)
        weave_scalar(c_bf[:, :, :2], picked[:])

        x1 = f32("x1", T)
        x2 = f32("x2", T)
        k_sum = f32("k_sum", 5)
        s_sum = f32("s_sum", 3)
        c0_ps = [ps.tile([P, BANK], F32, name="c0_ps%d" % h) for h in range(2)]
        for h, cols in enumerate(HALVES):
            product(c0_ps[h][:], go_codes[:], go_scales[:], cv_words[:, cols], cv_scales[:, cols])
            if h == 0:
                c0_sb = f32("c0_sb", BANK)
                x0 = f32("x0", BANK)
                nc.scalar.activation(out=c0_sb[:], in_=c0_ps[h][:], func=ACT.Copy)
                nc.gpsimd.tensor_tensor(out=x0[:], in0=c0_sb[:], in1=p[:, cols], op=ALU.mult)
                nc.scalar.activation(out=x1[:, cols], in_=x0[:], func=ACT.Copy, scale=neg_r[:], accum_out=s_sum[:, h:h + 1])
            else:
                nc.vector.scalar_tensor_tensor(out=x1[:, cols], in0=c0_ps[h][:], scalar=neg_r[:], in1=p[:, cols],
                                               op0=ALU.mult, op1=ALU.mult, accum_out=s_sum[:, h:h + 1])
            nc.scalar.activation(out=x2[:, cols], in_=x1[:, cols], func=ACT.Copy, scale=xzr[:], accum_out=k_sum[:, 2 + h:3 + h])

        for t in range(2, PACK):
            nc.vector.tensor_copy(out=c_bf[:, :, t], in_=planes[t][:].indirect(idx2[:]))
        c_codes = sb.tile([P, I], U32, name="c_codes", align_bytes=64)
        c_scales = sb.tile([P, I], U8, name="c_scales", align_bytes=64)
        quantize(c_codes[:], c_scales[:], c_bf[:])
        c1_ps = ps.tile([P, I], F32, name="c1_ps", tag="listed")
        product(c1_ps[:], go_codes[:], go_scales[:], c_codes[:], c_scales[:])
        y = sb.tile([P, T], F32, name="y", tag="c_bf", align_bytes=64)
        for h, cols in enumerate(HALVES):
            nc.vector.scalar_tensor_tensor(out=y[:, cols], in0=c0_ps[h][:], scalar=1.0, in1=xpr[:, cols],
                                           op0=ALU.mult, op1=ALU.mult, accum_out=k_sum[:, h:h + 1])
        xe1 = f32("xe1", I)
        nc.vector.scalar_tensor_tensor(out=xe1[:], in0=c1_ps[:], scalar=neg_r[:], in1=w_dir[:],
                                       op0=ALU.mult, op1=ALU.mult, accum_out=k_sum[:, 4:5])
        hv = f32("hv", I)
        nc.vector.scalar_tensor_tensor(out=hv[:], in0=c1_ps[:], scalar=neg_r[:], in1=w_val[:],
                                       op0=ALU.mult, op1=ALU.mult, accum_out=s_sum[:, 2:3])
        nc.vector.tensor_copy(out=xs1[:].indirect(idx[:]), in_=xe1[:])
        k_part = scaled_sum("k_part", k_sum[:], neg_r)
        f_xp = scaled_sum("f_xp", s_sum[:], big_r)
        f_p = f32("f_p", 1)
        nc.scalar.activation(out=f_p[:], in_=f_xp[:], func=ACT.Identity, scale=neg_mu[:], bias=k_part[:])
        e = f32("e", T)
        pe = f32("pe", T)
        for cols in HALVES:
            nc.scalar.activation(out=e[:, cols], in_=ta_sb[:, cols], func=ACT.Identity, scale=f_xp[:], bias=f_p[:])
            nc.gpsimd.tensor_tensor(out=pe[:, cols], in0=e[:, cols], in1=p[:, cols], op=ALU.mult)

        fixed_t = f32("fixed_t", T)
        fixed_ps = []
        for h, cols in enumerate(HALVES):
            turned = ps.tile([P, BANK], F32, name="turned%d" % h, tag="a_ps%d" % h)
            for b in range(BANK // P):
                local = slice(b * P, (b + 1) * P)
                block = slice(cols.start + b * P, cols.start + (b + 1) * P)
                for n, term in enumerate((y[:, block], x2[:, block], base_sb[:, block])):
                    nc.tensor.matmul(turned[:, local], term, ident[:],
                                     start=(n == 0), stop=(n == 2), is_transpose=True)
            nc.scalar.activation(out=fixed_t[:, cols], in_=turned[:], func=ACT.Copy)
        for h, cols in enumerate(HALVES):
            back = ps.tile([P, BANK], F32, name="back%d" % h, tag="ta_ps%d" % h)
            for b in range(BANK // P):
                block = slice(cols.start + b * P, cols.start + (b + 1) * P)
                nc.tensor.transpose(back[:, b * P:(b + 1) * P], fixed_t[:, block], ident[:])
            fixed_ps.append(back)

        t1 = f32("t1", T)
        res = f32("res", T)
        for h, cols in enumerate(HALVES):
            nc.vector.tensor_tensor(out=t1[:, cols], in0=fixed_ps[h][:], in1=xs1[:, cols], op=ALU.add)
        for n, (c0, w) in enumerate(STORE_PIECES):
            cols = slice(c0, c0 + w)
            nc.vector.tensor_tensor(out=res[:, cols], in0=t1[:, cols], in1=pe[:, cols], op=ALU.add)
            (nc.sync, nc.scalar)[n % 2].dma_start(out=out[:, cols], in_=res[:, cols])
